import numpy as np
import ml_dtypes


def mxq(x, axis, fmt="e4m3"):
    dtype, down = {"e4m3": (ml_dtypes.float8_e4m3fn, 7), "e5m2": (ml_dtypes.float8_e5m2, 14)}[fmt]
    v = np.moveaxis(np.asarray(x, np.float32).astype(ml_dtypes.bfloat16).astype(np.float64), axis, -1)
    blocks = v.reshape(v.shape[:-1] + (-1, 32))
    amax = np.abs(blocks).max(-1, keepdims=True)
    byte = np.maximum(np.where(amax > 0, np.frexp(amax)[1] - 1 + 127, 0) - down, 1)
    scale = np.exp2(byte - 127.0)
    codes = (blocks / scale).astype(np.float32).astype(dtype).astype(np.float64)
    return np.moveaxis((codes * scale).reshape(v.shape), -1, axis)


WIDE = False


def mx_kscale(k):
    if not WIDE:
        return np.ones(k)
    levels = np.array([10, -10, 5, -5, 0])
    if k % 512:
        return np.exp2(np.random.permutation(np.resize(levels, k // 32))).repeat(32)
    a = np.empty((k // 512, 16))
    for p in range(k // 512):
        a[p, :8] = np.random.permutation(np.resize(levels, 8))
        for g in range(8):
            far = levels[np.abs(levels - a[p, g]) >= 10]
            a[p, g + 8] = far[np.random.randint(len(far))]
    return np.exp2(a.ravel()).repeat(32)


def f64(x):
    return np.asarray(x).astype(np.float64)


def striped(idx):
    return np.tile(idx.reshape(-1, 16).T, (8, 1)).astype(np.uint16)


def unstriped(offs):
    return offs[:16].T.reshape(-1).astype(np.int64)


def striped8(idx):
    return np.concatenate([x.reshape(-1, 16).T for x in idx]).astype(np.uint16)


def runs(offs, k):
    lists = np.stack([offs[16 * r : 16 * r + 16].T.reshape(-1) for r in range(8)]).astype(np.int64)
    return lists[np.arange(k) % 512 // 64]


def pack_weight(w):
    k, n = w.shape
    w = f64(np.asarray(w, np.float32).astype(ml_dtypes.bfloat16)).reshape(k // 32, 32, n)
    amax = np.abs(w).max(1)
    byte = np.clip(np.where(amax > 0, np.frexp(amax)[1] - 1 + 127 - 7, 1), 1, 254)
    scaled = (w * np.exp2(127.0 - byte)[:, None, :]).reshape(k, n).astype(np.float32)
    words = np.ascontiguousarray(scaled.reshape(k // 512, 128, 4, n).transpose(0, 1, 3, 2)).astype(ml_dtypes.float8_e4m3fn).view(np.uint8)
    return words, np.ascontiguousarray(byte.astype(np.uint8).reshape(k // 512, 16, n))


def unpack_weight(words, scales):
    g, p, n, _ = words.shape
    vals = np.ascontiguousarray(words).view(ml_dtypes.float8_e4m3fn).astype(np.float64) * np.repeat(np.exp2(scales.astype(np.float64) - 127.0), 8, axis=1)[..., None]
    return vals.transpose(0, 1, 3, 2).reshape(g * 512, n)


def sigmoid(v):
    return 1.0 / (1.0 + np.exp(-np.maximum(v, -700.0)))


K, T, S, N, H, U = 512, 2048, 512, 512, 512, 1024


def setup_inputs():
    n = np.random.standard_normal
    s = mx_kscale(K)[:, None]
    u = mx_kscale(H)
    packed_xT = pack_weight(n((K, T)) * s)
    return {
        "x_words": packed_xT[0],
        "x_scales": packed_xT[1],
        "w1": (n((K, H)) / np.sqrt(K) / s).astype(np.float32),
        "gn": (np.random.uniform(0.5, 1.5, (H, 1)) * u[:, None]).astype(np.float32),
        "w2": (n((H, N)) / np.sqrt(H) / u[:, None]).astype(np.float32),
        "mem": n((N, U)).astype(np.float32),
        "offs": striped(np.random.permutation(T)[:S]),
        "c1": striped8(np.stack([np.random.permutation(S) for _ in range(8)])),
        "c2": striped8(np.stack([np.random.permutation(S) for _ in range(8)])),
        "c3": striped8(np.stack([np.random.permutation(S) for _ in range(8)])),
        "slot": striped8(np.stack([np.random.permutation(U)[:S] for _ in range(8)])),
    }


def reference(x_words, x_scales, w1, gn, w2, mem, offs, c1, c2, c3, slot):
    xq = unpack_weight(x_words, x_scales)[:, unstriped(offs)]
    p = sigmoid(mxq(f64(w1), 0, "e4m3").T @ xq)
    a = p[np.arange(H)[:, None], runs(c1, H)]
    b = p[np.arange(H)[:, None], runs(c2, H)]
    c = p[np.arange(H)[:, None], runs(c3, H)]
    z = f64(gn) * ((-1.0 * a + 1) * (-1.0 * b + 1) - (a * c))
    h = mxq(f64(w2), 0, "e4m3").T @ mxq(z, 0, "e4m3")
    out = f64(mem).copy()
    out[np.arange(N)[:, None], runs(slot, N)] = h
    return out

@@ -1,0 +1,150 @@
+from contextlib import ExitStack
+
+import concourse.mybir as mybir
+from concourse.masks import make_identity
+
+K, T, S, N, H, U = 512, 2048, 512, 512, 512, 1024
+FLOPS = 2 * K * H * S + 2 * H * N * S
+
+F32 = mybir.dt.float32
+BF16 = mybir.dt.bfloat16
+I32 = mybir.dt.int32
+U32 = mybir.dt.uint32
+U16 = mybir.dt.uint16
+U8 = mybir.dt.uint8
+FP8X4 = mybir.dt.float8_e4m3fn_x4
+ALU = mybir.AluOpType
+ACT = mybir.ActivationFunctionType
+
+P = 128
+PACK = 4
+W = 128
+SLICES = S // W
+COLS = W // 16
+
+
+def tile_picked_noisygate_none_p_kernel(tc, x_words, x_scales, w1, gn, w2, mem, offs, c1, c2, c3, slot, out):
+    nc = tc.nc
+    with ExitStack() as ctx:
+        keep = ctx.enter_context(tc.tile_pool(name="keep", bufs=1))
+        ring = ctx.enter_context(tc.tile_pool(name="ring", bufs=2))
+        psum = ctx.enter_context(tc.psum_pool(name="psum", bufs=1))
+        psum_h = ctx.enter_context(tc.psum_pool(name="psum_h", bufs=2))
+
+        def load_list(src, name):
+            lst = keep.tile([P, S // 16], U16, name=name)
+            nc.sync.dma_start(lst[:], src)
+            return lst
+
+        x_scale_rows = keep.tile([P, T], U8, align_bytes=64)
+        nc.vector.memset(x_scale_rows[:].bitcast(I32), 0)
+        offs_sb = load_list(offs, "offs_sb")
+        w1_raw = keep.tile([P, PACK, H], F32)
+        nc.sync.dma_start(out=w1_raw[:], in_=w1.rearrange("(p j) c -> p j c", j=PACK))
+        for q in range(4):
+            nc.sync.dma_start(out=x_scale_rows[32 * q : 32 * q + 4, :].bitcast(I32), in_=x_scales[0, 4 * q : 4 * q + 4, :].bitcast(I32))
+        x_word_cols = keep.tile([P, T], I32, align_bytes=64)
+        nc.sync.dma_start(out=x_word_cols[:], in_=x_words[0].rearrange("p n t -> p (n t)").bitcast(I32))
+        c2_sb = load_list(c2, "c2_sb")
+        c3_sb = load_list(c3, "c3_sb")
+        c1_sb = load_list(c1, "c1_sb")
+        gn_row = keep.tile([P, H], F32)
+        nc.gpsimd.memset(gn_row[:], 0.0)
+        nc.sync.dma_start(out=gn_row[0:1, :], in_=gn.rearrange("h o -> o h"))
+        w2_raw = ring.tile([P, PACK, N], F32, tag="picked")
+        nc.sync.dma_start(out=w2_raw[:], in_=w2.rearrange("(p j) c -> p j c", j=PACK))
+        slot_sb = load_list(slot, "slot_sb")
+        mem_rows = mem.rearrange("(p t) u -> p t u", t=PACK)
+        out_rows = out.rearrange("(p t) u -> p t u", t=PACK)
+        pages = []
+        for t in range(PACK):
+            page = keep.tile([P, U], F32, name="page%d" % t)
+            nc.sync.dma_start(out=page[:], in_=mem_rows[:, t, :])
+            pages.append(page)
+
+        def quantise_weight(raw, name, split):
+            grouped = keep.tile([P, PACK, P, PACK], BF16, name=name + "_bf16", tag="w1_bf16" if split else "turn", align_bytes=64)
+            dst = grouped[:].rearrange("p t m j -> p m j t")
+            src = raw[:].rearrange("p j (m t) -> p m j t", t=PACK)
+            if split:
+                nc.scalar.copy(out=dst[:, :split], in_=src[:, :split])
+                nc.vector.tensor_copy(out=dst[:, split:], in_=src[:, split:])
+            else:
+                nc.vector.tensor_copy(out=dst, in_=src)
+            codes = keep.tile([P, PACK * P], U32, name=name + "_codes", tag="turn" if split else "w2_codes", align_bytes=64)
+            scales = keep.tile([P, PACK * P], U8, name=name + "_scales", align_bytes=64)
+            nc.vector.quantize_mx(out=codes[:].bitcast(FP8X4), scales=scales[:], in_=grouped[:].rearrange("p t m j -> p (t m j)"))
+            return codes, scales
+
+        xs = keep.tile([P, S], U8, align_bytes=64)
+        nc.vector.tensor_copy(out=xs[:], in_=x_scale_rows[:].indirect(offs_sb[:]))
+        w1_codes, w1_scales = quantise_weight(w1_raw, "w1", 48)
+        xw = keep.tile([P, S], U32, align_bytes=64)
+        nc.vector.tensor_copy(out=xw[:], in_=x_word_cols[:].bitcast(U32).indirect(offs_sb[:]))
+
+        identity = keep.tile([P, P], F32)
+        make_identity(nc, identity[:])
+        gn_bank = psum.tile([P, PACK, P], F32, name="gn_bank")
+        for t in range(PACK):
+            nc.tensor.transpose(gn_bank[:, t, :], gn_row[:, t::PACK], identity[:])
+
+        ys = []
+        for t in range(PACK):
+            acc = psum.tile([P, S], F32, name="y_acc%d" % t)
+            cols = slice(t * P, (t + 1) * P)
+            nc.tensor.matmul_mx(out=acc[:], lhsT=w1_codes[:, cols].bitcast(FP8X4), lhsT_scale=w1_scales[:, cols],
+                                rhs=xw[:].bitcast(FP8X4), rhs_scale=xs[:], start=True, stop=True)
+            y = keep.tile([P, S], F32, name="y%d" % t)
+            nc.vector.tensor_copy(out=y[:], in_=acc[:])
+            ys.append(y)
+
+        w2_codes, w2_scales = quantise_weight(w2_raw, "w2", 0)
+
+        hs = [keep.tile([P, PACK - 1, W], F32, name="h%d" % s) for s in range(SLICES)]
+        shared = keep.tile([P, 2 * W], F32, align_bytes=64)
+        gain = gn_bank[:, :, 0:1].unsqueeze(1).broadcast_to([P, W // 4, PACK, 4])
+
+        def put(s, t, src):
+            nc.vector.tensor_copy(out=pages[t][:].indirect(slot_sb[:, s * COLS : (s + 1) * COLS]), in_=src)
+            if s == SLICES - 1:
+                nc.sync.dma_start(out=out_rows[:, t, :], in_=pages[t][:])
+
+        def put_last_tile(s, acc):
+            nc.vector.tensor_copy(out=shared[:, :W], in_=acc[:, PACK - 1, :])
+            put(s, PACK - 1, shared[:, :W])
+
+        accs = []
+        for s in range(SLICES):
+            cols = slice(s * COLS, (s + 1) * COLS)
+            picked = ring.tile([P, 3, PACK, W], F32, tag="picked")
+            nb, c, a = picked[:, 0], picked[:, 1], picked[:, 2]
+            u = keep.tile([P, PACK, W], F32, name="u")
+            gate_engine = nc.vector if s == 0 else nc.gpsimd
+            d = ring.tile([P, PACK, W], F32, name="d")
+            for t in range(PACK):
+                nc.scalar.activation(nb[:, t, :], ys[t][:].indirect(c2_sb[:, cols]), ACT.Sigmoid, scale=-1.0)
+                nc.scalar.activation(c[:, t, :], ys[t][:].indirect(c3_sb[:, cols]), ACT.Sigmoid)
+            gate_engine.tensor_tensor(out=u[:], in0=nb, in1=c, op=ALU.add)
+            for half in (slice(0, 2), slice(2, 4)):
+                for t in range(half.start, half.stop):
+                    nc.scalar.activation(a[:, t, :], ys[t][:].indirect(c1_sb[:, cols]), ACT.Sigmoid)
+                gate_engine.tensor_tensor(out=u[:, half, :], in0=a[:, half, :], in1=u[:, half, :], op=ALU.mult)
+                gate_engine.tensor_tensor(out=d[:, half, :], in0=nb[:, half, :], in1=u[:, half, :], op=ALU.subtract)
+            z = shared[:].bitcast(BF16)
+            nc.vector.tensor_tensor(out=z.rearrange("p (g i t) -> p g t i", i=4, t=PACK), in0=d[:].rearrange("p t (g i) -> p g t i", i=4),
+                                    in1=gain, op=ALU.mult)
+            z_codes = ring.tile([P, W], U32, name="z_codes", align_bytes=64)
+            z_scales = ring.tile([P, W], U8, name="z_scales", align_bytes=64)
+            nc.vector.quantize_mx(out=z_codes[:].bitcast(FP8X4), scales=z_scales[:], in_=z)
+            acc = psum_h.tile([P, PACK, W], F32, name="h_acc")
+            accs.append(acc)
+            for t in range(PACK):
+                wc = slice(t * P, (t + 1) * P)
+                nc.tensor.matmul_mx(out=acc[:, t, :], lhsT=w2_codes[:, wc].bitcast(FP8X4), lhsT_scale=w2_scales[:, wc],
+                                    rhs=z_codes[:].bitcast(FP8X4), rhs_scale=z_scales[:], start=True, stop=True)
+            if s > 0:
+                put_last_tile(s - 1, accs[s - 1])
+            nc.vector.tensor_copy(out=hs[s][:], in_=acc[:, : PACK - 1, :])
+            for t in range(PACK - 1):
+                put(s, t, hs[s][:, t, :])
+        put_last_tile(SLICES - 1, accs[-1])

@@ -1,7 +1,6 @@
 from contextlib import ExitStack
 
 import concourse.mybir as mybir
-from concourse.masks import make_identity
 
 K, T, S, N, H, U = 512, 2048, 512, 512, 512, 1024
 FLOPS = 2 * K * H * S + 2 * H * N * S
@@ -45,14 +44,16 @@ def tile_picked_noisygate_none_p_kernel(tc, x_words, x_scales, w1, gn, w2, mem, 
             nc.sync.dma_start(out=x_scale_rows[32 * q : 32 * q + 4, :].bitcast(I32), in_=x_scales[0, 4 * q : 4 * q + 4, :].bitcast(I32))
         x_word_cols = keep.tile([P, T], I32, align_bytes=64)
         nc.sync.dma_start(out=x_word_cols[:], in_=x_words[0].rearrange("p n t -> p (n t)").bitcast(I32))
+        w2_rows = w2.rearrange("(p j) c -> p j c", j=PACK)
+        w2_low = keep.tile([P, PACK, N // 2], F32)
+        nc.sync.dma_start(out=w2_low[:], in_=w2_rows[:, :, : N // 2])
         c2_sb = load_list(c2, "c2_sb")
         c3_sb = load_list(c3, "c3_sb")
         c1_sb = load_list(c1, "c1_sb")
-        gn_row = keep.tile([P, H], F32)
-        nc.gpsimd.memset(gn_row[:], 0.0)
-        nc.sync.dma_start(out=gn_row[0:1, :], in_=gn.rearrange("h o -> o h"))
-        w2_raw = ring.tile([P, PACK, N], F32, tag="picked")
-        nc.sync.dma_start(out=w2_raw[:], in_=w2.rearrange("(p j) c -> p j c", j=PACK))
+        gn_sb = keep.tile([P, PACK], F32)
+        nc.sync.dma_start(out=gn_sb[:], in_=gn.rearrange("(p t) o -> p (t o)", t=PACK))
+        w2_high = keep.tile([P, PACK, N // 2], F32, tag="picked")
+        nc.sync.dma_start(out=w2_high[:], in_=w2_rows[:, :, N // 2 :])
         slot_sb = load_list(slot, "slot_sb")
         mem_rows = mem.rearrange("(p t) u -> p t u", t=PACK)
         out_rows = out.rearrange("(p t) u -> p t u", t=PACK)
@@ -62,31 +63,29 @@ def tile_picked_noisygate_none_p_kernel(tc, x_words, x_scales, w1, gn, w2, mem, 
             nc.sync.dma_start(out=page[:], in_=mem_rows[:, t, :])
             pages.append(page)
 
-        def quantise_weight(raw, name, split):
-            grouped = keep.tile([P, PACK, P, PACK], BF16, name=name + "_bf16", tag="w1_bf16" if split else "turn", align_bytes=64)
-            dst = grouped[:].rearrange("p t m j -> p m j t")
-            src = raw[:].rearrange("p j (m t) -> p m j t", t=PACK)
-            if split:
-                nc.scalar.copy(out=dst[:, :split], in_=src[:, :split])
-                nc.vector.tensor_copy(out=dst[:, split:], in_=src[:, split:])
-            else:
-                nc.vector.tensor_copy(out=dst, in_=src)
-            codes = keep.tile([P, PACK * P], U32, name=name + "_codes", tag="turn" if split else "w2_codes", align_bytes=64)
+        def grouped_view(grouped):
+            return grouped.rearrange("p (t m j) -> p m j t", t=PACK, j=PACK)
+
+        def dealt_view(raw):
+            return raw.rearrange("p j (m t) -> p m j t", t=PACK)
+
+        def quantise(grouped, name, tag):
+            codes = keep.tile([P, PACK * P], U32, name=name + "_codes", tag=tag, align_bytes=64)
             scales = keep.tile([P, PACK * P], U8, name=name + "_scales", align_bytes=64)
-            nc.vector.quantize_mx(out=codes[:].bitcast(FP8X4), scales=scales[:], in_=grouped[:].rearrange("p t m j -> p (t m j)"))
+            nc.vector.quantize_mx(out=codes[:].bitcast(FP8X4), scales=scales[:], in_=grouped)
             return codes, scales
 
         xs = keep.tile([P, S], U8, align_bytes=64)
         nc.vector.tensor_copy(out=xs[:], in_=x_scale_rows[:].indirect(offs_sb[:]))
-        w1_codes, w1_scales = quantise_weight(w1_raw, "w1", 48)
+        w1_bf16 = keep.tile([P, PACK * H], BF16, align_bytes=64)
+        nc.scalar.copy(out=grouped_view(w1_bf16[:])[:, :48], in_=dealt_view(w1_raw[:])[:, :48])
+        nc.vector.tensor_copy(out=grouped_view(w1_bf16[:])[:, 48:], in_=dealt_view(w1_raw[:])[:, 48:])
+        w1_codes, w1_scales = quantise(w1_bf16[:], "w1", "w1_codes")
         xw = keep.tile([P, S], U32, align_bytes=64)
         nc.vector.tensor_copy(out=xw[:], in_=x_word_cols[:].bitcast(U32).indirect(offs_sb[:]))
 
-        identity = keep.tile([P, P], F32)
-        make_identity(nc, identity[:])
-        gn_bank = psum.tile([P, PACK, P], F32, name="gn_bank")
-        for t in range(PACK):
-            nc.tensor.transpose(gn_bank[:, t, :], gn_row[:, t::PACK], identity[:])
+        w2_bf16 = keep.tile([P, PACK * N], BF16, align_bytes=64)
+        nc.vector.tensor_copy(out=grouped_view(w2_bf16[:])[:, : P // 2], in_=dealt_view(w2_low[:]))
 
         ys = []
         for t in range(PACK):
@@ -98,53 +97,104 @@ def tile_picked_noisygate_none_p_kernel(tc, x_words, x_scales, w1, gn, w2, mem, 
             nc.vector.tensor_copy(out=y[:], in_=acc[:])
             ys.append(y)
 
-        w2_codes, w2_scales = quantise_weight(w2_raw, "w2", 0)
+        nc.vector.tensor_copy(out=grouped_view(w2_bf16[:])[:, P // 2 :], in_=dealt_view(w2_high[:]))
+        w2_codes, w2_scales = quantise(w2_bf16[:], "w2", "w2_codes")
 
-        hs = [keep.tile([P, PACK - 1, W], F32, name="h%d" % s) for s in range(SLICES)]
-        shared = keep.tile([P, 2 * W], F32, align_bytes=64)
-        gain = gn_bank[:, :, 0:1].unsqueeze(1).broadcast_to([P, W // 4, PACK, 4])
+        last = SLICES - 1
+        first_picked = keep.tile([P, 1, 3, PACK, W], F32)
+        later_picked = keep.tile([P, last, 3, PACK, W], F32, tag="picked")
+
+        def picked(kind, step):
+            s, t = divmod(step, PACK)
+            return first_picked[:, 0, kind, t, :] if s == 0 else later_picked[:, s - 1, kind, t, :]
+
+        nbgs = [keep.tile([P, PACK, W], F32, name="nbg%d" % s) for s in range(SLICES)]
+
+        def gather(kind, lst, step, sign):
+            s, t = divmod(step, PACK)
+            nc.scalar.activation(picked(kind, step), ys[t][:].indirect(lst[:, s * COLS : (s + 1) * COLS]), ACT.Sigmoid, scale=sign)
+
+        def gain(step):
+            s, t = divmod(step, PACK)
+            if s == 0:
+                nc.vector.tensor_scalar(out=nbgs[s][:, t, :], in0=picked(0, step), scalar1=gn_sb[:, t : t + 1], scalar2=None, op0=ALU.mult)
+            else:
+                nc.scalar.activation(nbgs[s][:, t, :], picked(0, step), ACT.Copy, scale=gn_sb[:, t : t + 1])
+
+        accs = []
+
+        def copy_out(s, t, dst):
+            if s < last - 1:
+                nc.vector.tensor_copy(out=dst, in_=accs[s][:, t, :])
+            else:
+                nc.scalar.copy(out=dst, in_=accs[s][:, t, :])
 
         def put(s, t, src):
             nc.vector.tensor_copy(out=pages[t][:].indirect(slot_sb[:, s * COLS : (s + 1) * COLS]), in_=src)
-            if s == SLICES - 1:
+            if s == last:
                 nc.sync.dma_start(out=out_rows[:, t, :], in_=pages[t][:])
 
-        def put_last_tile(s, acc):
-            nc.vector.tensor_copy(out=shared[:, :W], in_=acc[:, PACK - 1, :])
-            put(s, PACK - 1, shared[:, :W])
-
-        accs = []
+        gather(0, c2_sb, 0, -1.0)
+        gain(0)
+        freed = None
         for s in range(SLICES):
-            cols = slice(s * COLS, (s + 1) * COLS)
-            picked = ring.tile([P, 3, PACK, W], F32, tag="picked")
-            nb, c, a = picked[:, 0], picked[:, 1], picked[:, 2]
-            u = keep.tile([P, PACK, W], F32, name="u")
-            gate_engine = nc.vector if s == 0 else nc.gpsimd
-            d = ring.tile([P, PACK, W], F32, name="d")
+            m = keep.tile([P, PACK, W], F32, name="m%d" % s)
+            z = keep.tile([P, 2 * W], F32, name="z%d" % s, align_bytes=64)
+            woven = 0 < s < last
+            waiting = []
+
+            def hand_on(t, dst):
+                while waiting:
+                    put(*waiting.pop())
+                if dst is not None:
+                    copy_out(s - 1, t, dst)
+                    waiting.append((s - 1, t, dst))
+
             for t in range(PACK):
-                nc.scalar.activation(nb[:, t, :], ys[t][:].indirect(c2_sb[:, cols]), ACT.Sigmoid, scale=-1.0)
-                nc.scalar.activation(c[:, t, :], ys[t][:].indirect(c3_sb[:, cols]), ACT.Sigmoid)
-            gate_engine.tensor_tensor(out=u[:], in0=nb, in1=c, op=ALU.add)
-            for half in (slice(0, 2), slice(2, 4)):
-                for t in range(half.start, half.stop):
-                    nc.scalar.activation(a[:, t, :], ys[t][:].indirect(c1_sb[:, cols]), ACT.Sigmoid)
-                gate_engine.tensor_tensor(out=u[:, half, :], in0=a[:, half, :], in1=u[:, half, :], op=ALU.mult)
-                gate_engine.tensor_tensor(out=d[:, half, :], in0=nb[:, half, :], in1=u[:, half, :], op=ALU.subtract)
-            z = shared[:].bitcast(BF16)
-            nc.vector.tensor_tensor(out=z.rearrange("p (g i t) -> p g t i", i=4, t=PACK), in0=d[:].rearrange("p t (g i) -> p g t i", i=4),
-                                    in1=gain, op=ALU.mult)
-            z_codes = ring.tile([P, W], U32, name="z_codes", align_bytes=64)
+                step = PACK * s + t
+                if step + 1 < PACK * SLICES:
+                    gather(0, c2_sb, step + 1, -1.0)
+                gather(1, c3_sb, step, 1.0)
+                gather(2, c1_sb, step, 1.0)
+                if step + 1 < PACK * SLICES:
+                    gain(step + 1)
+                c, a = picked(1, step), picked(2, step)
+                if s == 0:
+                    sg = c
+                elif t < PACK - 1:
+                    sg = freed[t]
+                else:
+                    spare = keep.tile([P, W], F32, tag="z_codes", align_bytes=64)
+                    sg = spare[:]
+                nc.vector.scalar_tensor_tensor(out=sg, in0=c, scalar=gn_sb[:, t : t + 1], in1=nbgs[s][:, t, :], op0=ALU.mult, op1=ALU.add)
+                if woven and t == 1:
+                    hand_on(0, picked(0, step))
+                elif s == last and t == PACK - 1:
+                    hand_on(0, c)
+                else:
+                    hand_on(0, None)
+                nc.vector.tensor_tensor(out=m[:, t, :], in0=a, in1=sg, op=ALU.mult)
+                if woven and t >= 1:
+                    hand_on(t, a)
+                elif s == last and t == PACK - 1:
+                    hand_on(1, a)
+            z_bf16 = z[:].bitcast(BF16)
+            nc.vector.tensor_tensor(out=z_bf16.rearrange("p (g i t) -> p g t i", i=4, t=PACK), in0=nbgs[s][:].rearrange("p t (g i) -> p g t i", i=4),
+                                    in1=m[:].rearrange("p t (g i) -> p g t i", i=4), op=ALU.subtract)
+            hand_on(2, m[:, 0, :] if s == last else None)
+            z_codes = keep.tile([P, W], U32, tag="z_codes", align_bytes=64)
             z_scales = ring.tile([P, W], U8, name="z_scales", align_bytes=64)
-            nc.vector.quantize_mx(out=z_codes[:].bitcast(FP8X4), scales=z_scales[:], in_=z)
+            nc.vector.quantize_mx(out=z_codes[:].bitcast(FP8X4), scales=z_scales[:], in_=z_bf16)
             acc = psum_h.tile([P, PACK, W], F32, name="h_acc")
             accs.append(acc)
             for t in range(PACK):
                 wc = slice(t * P, (t + 1) * P)
                 nc.tensor.matmul_mx(out=acc[:, t, :], lhsT=w2_codes[:, wc].bitcast(FP8X4), lhsT_scale=w2_scales[:, wc],
                                     rhs=z_codes[:].bitcast(FP8X4), rhs_scale=z_scales[:], start=True, stop=True)
-            if s > 0:
-                put_last_tile(s - 1, accs[s - 1])
-            nc.vector.tensor_copy(out=hs[s][:], in_=acc[:, : PACK - 1, :])
-            for t in range(PACK - 1):
-                put(s, t, hs[s][:, t, :])
-        put_last_tile(SLICES - 1, accs[-1])
+            hand_on(3, z[:, :W] if s == last else None)
+            hand_on(3, None)
+            freed = [m[:, 0, :], z[:, :W], z[:, W:]]
+        for t in range(PACK):
+            dst = nbgs[last][:, t, :]
+            copy_out(last, t, dst)
+            put(last, t, dst)

@@ -20,6 +20,7 @@ PACK = 4
 W = 128
 SLICES = S // W
 COLS = W // 16
+LAG = (0, 0, 1, 3)
 
 
 def tile_picked_noisygate_none_p_kernel(tc, x_words, x_scales, w1, gn, w2, mem, offs, c1, c2, c3, slot, out):
@@ -78,37 +79,48 @@ def tile_picked_noisygate_none_p_kernel(tc, x_words, x_scales, w1, gn, w2, mem, 
         xs = keep.tile([P, S], U8, align_bytes=64)
         nc.vector.tensor_copy(out=xs[:], in_=x_scale_rows[:].indirect(offs_sb[:]))
         w1_bf16 = keep.tile([P, PACK * H], BF16, align_bytes=64)
-        nc.scalar.copy(out=grouped_view(w1_bf16[:])[:, :48], in_=dealt_view(w1_raw[:])[:, :48])
-        nc.vector.tensor_copy(out=grouped_view(w1_bf16[:])[:, 48:], in_=dealt_view(w1_raw[:])[:, 48:])
+        nc.scalar.copy(out=grouped_view(w1_bf16[:])[:, :64], in_=dealt_view(w1_raw[:])[:, :64])
+        nc.vector.tensor_copy(out=grouped_view(w1_bf16[:])[:, 64:], in_=dealt_view(w1_raw[:])[:, 64:])
         w1_codes, w1_scales = quantise(w1_bf16[:], "w1", "w1_codes")
-        xw = keep.tile([P, S], U32, align_bytes=64)
-        nc.vector.tensor_copy(out=xw[:], in_=x_word_cols[:].bitcast(U32).indirect(offs_sb[:]))
+        halves = [slice(0, S // 2), slice(S // 2, S)]
+        xws = []
+        for i in range(2):
+            xw = keep.tile([P, S // 2], U32, name="xw%d" % i, align_bytes=64)
+            nc.vector.tensor_copy(out=xw[:], in_=x_word_cols[:].bitcast(U32).indirect(offs_sb[:, 16 * i : 16 * i + 16]))
+            xws.append(xw)
 
-        w2_bf16 = keep.tile([P, PACK * N], BF16, align_bytes=64)
-        nc.vector.tensor_copy(out=grouped_view(w2_bf16[:])[:, : P // 2], in_=dealt_view(w2_low[:]))
+        w2_stage = keep.tile([P, 2 * W + PACK * N // 2], F32, align_bytes=64)
+        w2_bf16 = w2_stage[:, 2 * W :].bitcast(BF16)
+        nc.vector.tensor_copy(out=grouped_view(w2_bf16)[:, : P // 2], in_=dealt_view(w2_low[:]))
 
         ys = []
         for t in range(PACK):
             acc = psum.tile([P, S], F32, name="y_acc%d" % t)
             cols = slice(t * P, (t + 1) * P)
-            nc.tensor.matmul_mx(out=acc[:], lhsT=w1_codes[:, cols].bitcast(FP8X4), lhsT_scale=w1_scales[:, cols],
-                                rhs=xw[:].bitcast(FP8X4), rhs_scale=xs[:], start=True, stop=True)
+            for half, xw in zip(halves, xws):
+                nc.tensor.matmul_mx(out=acc[:, half], lhsT=w1_codes[:, cols].bitcast(FP8X4), lhsT_scale=w1_scales[:, cols],
+                                    rhs=xw[:].bitcast(FP8X4), rhs_scale=xs[:, half], start=True, stop=True)
             y = keep.tile([P, S], F32, name="y%d" % t)
             nc.vector.tensor_copy(out=y[:], in_=acc[:])
             ys.append(y)
 
-        nc.vector.tensor_copy(out=grouped_view(w2_bf16[:])[:, P // 2 :], in_=dealt_view(w2_high[:]))
-        w2_codes, w2_scales = quantise(w2_bf16[:], "w2", "w2_codes")
+        nc.vector.tensor_copy(out=grouped_view(w2_bf16)[:, P // 2 :], in_=dealt_view(w2_high[:]))
+        w2_codes, w2_scales = quantise(w2_bf16, "w2", "w2_codes")
 
         last = SLICES - 1
-        first_picked = keep.tile([P, 1, 3, PACK, W], F32)
-        later_picked = keep.tile([P, last, 3, PACK, W], F32, tag="picked")
+        picked_tiles = [keep.tile([P, 3, PACK, W], F32, name="picked0")[:]]
+        middle = keep.tile([P, 2, 3, PACK, W], F32, tag="picked")
+        picked_tiles.extend([middle[:, 0], middle[:, 1]])
 
         def picked(kind, step):
             s, t = divmod(step, PACK)
-            return first_picked[:, 0, kind, t, :] if s == 0 else later_picked[:, s - 1, kind, t, :]
+            return picked_tiles[s][:, kind, t, :]
 
-        nbgs = [keep.tile([P, PACK, W], F32, name="nbg%d" % s) for s in range(SLICES)]
+        nbgs = [w2_stage[:, : PACK * W].rearrange("p (t w) -> p t w", t=PACK)]
+        nbgs.extend([keep.tile([P, PACK, W], F32, name="nbg%d" % s)[:] for s in range(1, SLICES)])
+        m = keep.tile([P, PACK, W], F32)
+        z = keep.tile([P, 2 * W], F32, align_bytes=64)
+        z_bf16 = z[:].bitcast(BF16)
 
         def gather(kind, lst, step, sign):
             s, t = divmod(step, PACK)
@@ -124,10 +136,10 @@ def tile_picked_noisygate_none_p_kernel(tc, x_words, x_scales, w1, gn, w2, mem, 
         accs = []
 
         def copy_out(s, t, dst):
-            if s < last - 1:
-                nc.vector.tensor_copy(out=dst, in_=accs[s][:, t, :])
+            if s == 0:
+                nc.vector.tensor_copy(out=dst, in_=accs[s][t])
             else:
-                nc.scalar.copy(out=dst, in_=accs[s][:, t, :])
+                nc.scalar.copy(out=dst, in_=accs[s][t])
 
         def put(s, t, src):
             nc.vector.tensor_copy(out=pages[t][:].indirect(slot_sb[:, s * COLS : (s + 1) * COLS]), in_=src)
@@ -136,20 +148,21 @@ def tile_picked_noisygate_none_p_kernel(tc, x_words, x_scales, w1, gn, w2, mem, 
 
         gather(0, c2_sb, 0, -1.0)
         gain(0)
-        freed = None
         for s in range(SLICES):
-            m = keep.tile([P, PACK, W], F32, name="m%d" % s)
-            z = keep.tile([P, 2 * W], F32, name="z%d" % s, align_bytes=64)
-            woven = 0 < s < last
             waiting = []
 
-            def hand_on(t, dst):
+            def hand_on(place, dst):
                 while waiting:
-                    put(*waiting.pop())
-                if dst is not None:
+                    put(*waiting.pop(0))
+                t = place - LAG[s]
+                if s > 0 and 0 <= t < (PACK if s < last else PACK - 1):
                     copy_out(s - 1, t, dst)
                     waiting.append((s - 1, t, dst))
 
+            if s == 1:
+                spare = keep.tile([P, PACK - 1, W], F32, tag="codes0", align_bytes=64)
+            if s == last - 1:
+                picked_tiles.append(keep.tile([P, 3, PACK, W], F32, name="picked3", tag="codes1", align_bytes=64)[:])
             for t in range(PACK):
                 step = PACK * s + t
                 if step + 1 < PACK * SLICES:
@@ -159,42 +172,37 @@ def tile_picked_noisygate_none_p_kernel(tc, x_words, x_scales, w1, gn, w2, mem, 
                 if step + 1 < PACK * SLICES:
                     gain(step + 1)
                 c, a = picked(1, step), picked(2, step)
-                if s == 0:
-                    sg = c
-                elif t < PACK - 1:
-                    sg = freed[t]
-                else:
-                    spare = keep.tile([P, W], F32, tag="z_codes", align_bytes=64)
-                    sg = spare[:]
+                sg = spare[:, t - 1, :] if s == 1 and t > 0 else m[:, t, :]
                 nc.vector.scalar_tensor_tensor(out=sg, in0=c, scalar=gn_sb[:, t : t + 1], in1=nbgs[s][:, t, :], op0=ALU.mult, op1=ALU.add)
-                if woven and t == 1:
-                    hand_on(0, picked(0, step))
-                elif s == last and t == PACK - 1:
-                    hand_on(0, c)
+                if t == 0 and s > 0:
+                    hand_on(0, picked(0, step - PACK))
+                    hand_on(1, picked(0, step - PACK + 1))
                 else:
-                    hand_on(0, None)
+                    hand_on(-1, None)
                 nc.vector.tensor_tensor(out=m[:, t, :], in0=a, in1=sg, op=ALU.mult)
-                if woven and t >= 1:
-                    hand_on(t, a)
-                elif s == last and t == PACK - 1:
-                    hand_on(1, a)
-            z_bf16 = z[:].bitcast(BF16)
-            nc.vector.tensor_tensor(out=z_bf16.rearrange("p (g i t) -> p g t i", i=4, t=PACK), in0=nbgs[s][:].rearrange("p t (g i) -> p g t i", i=4),
+                hand_on(t + 1 if t > 0 else -1, a)
+            nc.vector.tensor_tensor(out=z_bf16.rearrange("p (g i t) -> p g t i", i=4, t=PACK), in0=nbgs[s].rearrange("p t (g i) -> p g t i", i=4),
                                     in1=m[:].rearrange("p t (g i) -> p g t i", i=4), op=ALU.subtract)
-            hand_on(2, m[:, 0, :] if s == last else None)
-            z_codes = keep.tile([P, W], U32, tag="z_codes", align_bytes=64)
+            hand_on(PACK + 1, nbgs[s][:, 0, :])
+            z_codes = keep.tile([P, W], U32, name="z_codes", tag="codes%d" % s, align_bytes=64)
             z_scales = ring.tile([P, W], U8, name="z_scales", align_bytes=64)
             nc.vector.quantize_mx(out=z_codes[:].bitcast(FP8X4), scales=z_scales[:], in_=z_bf16)
-            acc = psum_h.tile([P, PACK, W], F32, name="h_acc")
+            if s < last:
+                bank = psum_h.tile([P, PACK, W], F32, name="h_acc")
+                acc = [bank[:, t, :] for t in range(PACK)]
+            else:
+                acc = [psum.tile([P, W], F32, name="y_acc%d" % t)[:] for t in range(PACK)]
             accs.append(acc)
             for t in range(PACK):
                 wc = slice(t * P, (t + 1) * P)
-                nc.tensor.matmul_mx(out=acc[:, t, :], lhsT=w2_codes[:, wc].bitcast(FP8X4), lhsT_scale=w2_scales[:, wc],
+                nc.tensor.matmul_mx(out=acc[t], lhsT=w2_codes[:, wc].bitcast(FP8X4), lhsT_scale=w2_scales[:, wc],
                                     rhs=z_codes[:].bitcast(FP8X4), rhs_scale=z_scales[:], start=True, stop=True)
-            hand_on(3, z[:, :W] if s == last else None)
-            hand_on(3, None)
-            freed = [m[:, 0, :], z[:, :W], z[:, W:]]
+            hand_on(-1, None)
         for t in range(PACK):
-            dst = nbgs[last][:, t, :]
+            if t == PACK - 1:
+                late = picked(1, PACK * last)
+                copy_out(last - 1, t, late)
+                put(last - 1, t, late)
+            dst = picked(1, PACK * last + t)
             copy_out(last, t, dst)
             put(last, t, dst)

@@ -39,16 +39,16 @@ def tile_picked_noisygate_none_p_kernel(tc, x_words, x_scales, w1, gn, w2, mem, 
         x_scale_rows = keep.tile([P, T], U8, align_bytes=64)
         nc.vector.memset(x_scale_rows[:].bitcast(I32), 0)
         offs_sb = load_list(offs, "offs_sb")
-        w1_raw = keep.tile([P, PACK, H], F32)
-        nc.sync.dma_start(out=w1_raw[:], in_=w1.rearrange("(p j) c -> p j c", j=PACK))
+        c2_sb = load_list(c2, "c2_sb")
         for q in range(4):
             nc.sync.dma_start(out=x_scale_rows[32 * q : 32 * q + 4, :].bitcast(I32), in_=x_scales[0, 4 * q : 4 * q + 4, :].bitcast(I32))
+        w1_raw = keep.tile([P, PACK, H], F32)
+        nc.sync.dma_start(out=w1_raw[:], in_=w1.rearrange("(p j) c -> p j c", j=PACK))
         x_word_cols = keep.tile([P, T], I32, align_bytes=64)
         nc.sync.dma_start(out=x_word_cols[:], in_=x_words[0].rearrange("p n t -> p (n t)").bitcast(I32))
         w2_rows = w2.rearrange("(p j) c -> p j c", j=PACK)
         w2_low = keep.tile([P, PACK, N // 2], F32)
         nc.sync.dma_start(out=w2_low[:], in_=w2_rows[:, :, : N // 2])
-        c2_sb = load_list(c2, "c2_sb")
         c3_sb = load_list(c3, "c3_sb")
         c1_sb = load_list(c1, "c1_sb")
         gn_sb = keep.tile([P, PACK], F32)
@@ -79,8 +79,8 @@ def tile_picked_noisygate_none_p_kernel(tc, x_words, x_scales, w1, gn, w2, mem, 
         xs = keep.tile([P, S], U8, align_bytes=64)
         nc.vector.tensor_copy(out=xs[:], in_=x_scale_rows[:].indirect(offs_sb[:]))
         w1_bf16 = keep.tile([P, PACK * H], BF16, align_bytes=64)
-        nc.scalar.copy(out=grouped_view(w1_bf16[:])[:, :64], in_=dealt_view(w1_raw[:])[:, :64])
-        nc.vector.tensor_copy(out=grouped_view(w1_bf16[:])[:, 64:], in_=dealt_view(w1_raw[:])[:, 64:])
+        nc.scalar.copy(out=grouped_view(w1_bf16[:])[:, :48], in_=dealt_view(w1_raw[:])[:, :48])
+        nc.vector.tensor_copy(out=grouped_view(w1_bf16[:])[:, 48:], in_=dealt_view(w1_raw[:])[:, 48:])
         w1_codes, w1_scales = quantise(w1_bf16[:], "w1", "w1_codes")
         halves = [slice(0, S // 2), slice(S // 2, S)]
         xws = []

@@ -44,7 +44,7 @@ def tile_picked_noisygate_none_p_kernel(tc, x_words, x_scales, w1, gn, w2, mem, 
             nc.sync.dma_start(out=x_scale_rows[32 * q : 32 * q + 4, :].bitcast(I32), in_=x_scales[0, 4 * q : 4 * q + 4, :].bitcast(I32))
         w1_raw = keep.tile([P, PACK, H], F32)
         nc.sync.dma_start(out=w1_raw[:], in_=w1.rearrange("(p j) c -> p j c", j=PACK))
-        x_word_cols = keep.tile([P, T], I32, align_bytes=64)
+        x_word_cols = keep.tile([P, T], I32, tag="x_words", align_bytes=64)
         nc.sync.dma_start(out=x_word_cols[:], in_=x_words[0].rearrange("p n t -> p (n t)").bitcast(I32))
         w2_rows = w2.rearrange("(p j) c -> p j c", j=PACK)
         w2_low = keep.tile([P, PACK, N // 2], F32)
@@ -78,18 +78,16 @@ def tile_picked_noisygate_none_p_kernel(tc, x_words, x_scales, w1, gn, w2, mem, 
 
         xs = keep.tile([P, S], U8, align_bytes=64)
         nc.vector.tensor_copy(out=xs[:], in_=x_scale_rows[:].indirect(offs_sb[:]))
-        w1_bf16 = keep.tile([P, PACK * H], BF16, align_bytes=64)
-        nc.scalar.copy(out=grouped_view(w1_bf16[:])[:, :48], in_=dealt_view(w1_raw[:])[:, :48])
-        nc.vector.tensor_copy(out=grouped_view(w1_bf16[:])[:, 48:], in_=dealt_view(w1_raw[:])[:, 48:])
+        w1_bf16 = keep.tile([P, PACK * H], BF16, tag="w1_bf16", align_bytes=64)
+        nc.scalar.copy(out=grouped_view(w1_bf16[:])[:, :40], in_=dealt_view(w1_raw[:])[:, :40])
+        nc.vector.tensor_copy(out=grouped_view(w1_bf16[:])[:, 40:], in_=dealt_view(w1_raw[:])[:, 40:])
         w1_codes, w1_scales = quantise(w1_bf16[:], "w1", "w1_codes")
         halves = [slice(0, S // 2), slice(S // 2, S)]
-        xws = []
-        for i in range(2):
-            xw = keep.tile([P, S // 2], U32, name="xw%d" % i, align_bytes=64)
-            nc.vector.tensor_copy(out=xw[:], in_=x_word_cols[:].bitcast(U32).indirect(offs_sb[:, 16 * i : 16 * i + 16]))
-            xws.append(xw)
+        xw = keep.tile([P, S], U32, tag="w1_bf16", align_bytes=64)
+        for i, half in enumerate(halves):
+            nc.vector.tensor_copy(out=xw[:, half], in_=x_word_cols[:].bitcast(U32).indirect(offs_sb[:, 16 * i : 16 * i + 16]))
 
-        w2_stage = keep.tile([P, 2 * W + PACK * N // 2], F32, align_bytes=64)
+        w2_stage = keep.tile([P, 2 * W + PACK * N // 2], F32, tag="x_words", align_bytes=64)
         w2_bf16 = w2_stage[:, 2 * W :].bitcast(BF16)
         nc.vector.tensor_copy(out=grouped_view(w2_bf16)[:, : P // 2], in_=dealt_view(w2_low[:]))
 
@@ -97,9 +95,9 @@ def tile_picked_noisygate_none_p_kernel(tc, x_words, x_scales, w1, gn, w2, mem, 
         for t in range(PACK):
             acc = psum.tile([P, S], F32, name="y_acc%d" % t)
             cols = slice(t * P, (t + 1) * P)
-            for half, xw in zip(halves, xws):
+            for half in halves:
                 nc.tensor.matmul_mx(out=acc[:, half], lhsT=w1_codes[:, cols].bitcast(FP8X4), lhsT_scale=w1_scales[:, cols],
-                                    rhs=xw[:].bitcast(FP8X4), rhs_scale=xs[:, half], start=True, stop=True)
+                                    rhs=xw[:, half].bitcast(FP8X4), rhs_scale=xs[:, half], start=True, stop=True)
             y = keep.tile([P, S], F32, name="y%d" % t)
             nc.vector.tensor_copy(out=y[:], in_=acc[:])
             ys.append(y)

from contextlib import ExitStack

import concourse.mybir as mybir

K, T, S, N, H, U = 512, 2048, 512, 512, 512, 1024
FLOPS = 2 * K * H * S + 2 * H * N * S

F32 = mybir.dt.float32
BF16 = mybir.dt.bfloat16
I32 = mybir.dt.int32
U32 = mybir.dt.uint32
U16 = mybir.dt.uint16
U8 = mybir.dt.uint8
FP8X4 = mybir.dt.float8_e4m3fn_x4
ALU = mybir.AluOpType
ACT = mybir.ActivationFunctionType

P = 128
PACK = 4
W = 128
SLICES = S // W
COLS = W // 16
LAG = (0, 0, 1, 3)


def tile_picked_noisygate_none_p_kernel(tc, x_words, x_scales, w1, gn, w2, mem, offs, c1, c2, c3, slot, out):
    nc = tc.nc
    with ExitStack() as ctx:
        keep = ctx.enter_context(tc.tile_pool(name="keep", bufs=1))
        ring = ctx.enter_context(tc.tile_pool(name="ring", bufs=2))
        psum = ctx.enter_context(tc.psum_pool(name="psum", bufs=1))
        psum_h = ctx.enter_context(tc.psum_pool(name="psum_h", bufs=2))

        def load_list(src, name):
            lst = keep.tile([P, S // 16], U16, name=name)
            nc.sync.dma_start(lst[:], src)
            return lst

        x_scale_rows = keep.tile([P, T], U8, align_bytes=64)
        nc.vector.memset(x_scale_rows[:].bitcast(I32), 0)
        offs_sb = load_list(offs, "offs_sb")
        c2_sb = load_list(c2, "c2_sb")
        for q in range(4):
            nc.sync.dma_start(out=x_scale_rows[32 * q : 32 * q + 4, :].bitcast(I32), in_=x_scales[0, 4 * q : 4 * q + 4, :].bitcast(I32))
        w1_raw = keep.tile([P, PACK, H], F32)
        nc.sync.dma_start(out=w1_raw[:], in_=w1.rearrange("(p j) c -> p j c", j=PACK))
        x_word_cols = keep.tile([P, T], I32, tag="x_words", align_bytes=64)
        nc.sync.dma_start(out=x_word_cols[:], in_=x_words[0].rearrange("p n t -> p (n t)").bitcast(I32))
        w2_rows = w2.rearrange("(p j) c -> p j c", j=PACK)
        w2_low = keep.tile([P, PACK, N // 2], F32)
        nc.sync.dma_start(out=w2_low[:], in_=w2_rows[:, :, : N // 2])
        c3_sb = load_list(c3, "c3_sb")
        c1_sb = load_list(c1, "c1_sb")
        gn_sb = keep.tile([P, PACK], F32)
        nc.sync.dma_start(out=gn_sb[:], in_=gn.rearrange("(p t) o -> p (t o)", t=PACK))
        w2_high = keep.tile([P, PACK, N // 2], F32, tag="picked")
        nc.sync.dma_start(out=w2_high[:], in_=w2_rows[:, :, N // 2 :])
        slot_sb = load_list(slot, "slot_sb")
        mem_rows = mem.rearrange("(p t) u -> p t u", t=PACK)
        out_rows = out.rearrange("(p t) u -> p t u", t=PACK)
        pages = []
        for t in range(PACK):
            page = keep.tile([P, U], F32, name="page%d" % t)
            nc.sync.dma_start(out=page[:], in_=mem_rows[:, t, :])
            pages.append(page)

        def grouped_view(grouped):
            return grouped.rearrange("p (t m j) -> p m j t", t=PACK, j=PACK)

        def dealt_view(raw):
            return raw.rearrange("p j (m t) -> p m j t", t=PACK)

        def quantise(grouped, name, tag):
            codes = keep.tile([P, PACK * P], U32, name=name + "_codes", tag=tag, align_bytes=64)
            scales = keep.tile([P, PACK * P], U8, name=name + "_scales", align_bytes=64)
            nc.vector.quantize_mx(out=codes[:].bitcast(FP8X4), scales=scales[:], in_=grouped)
            return codes, scales

        xs = keep.tile([P, S], U8, align_bytes=64)
        nc.vector.tensor_copy(out=xs[:], in_=x_scale_rows[:].indirect(offs_sb[:]))
        w1_bf16 = keep.tile([P, PACK * H], BF16, tag="w1_bf16", align_bytes=64)
        nc.scalar.copy(out=grouped_view(w1_bf16[:])[:, :40], in_=dealt_view(w1_raw[:])[:, :40])
        nc.vector.tensor_copy(out=grouped_view(w1_bf16[:])[:, 40:], in_=dealt_view(w1_raw[:])[:, 40:])
        w1_codes, w1_scales = quantise(w1_bf16[:], "w1", "w1_codes")
        halves = [slice(0, S // 2), slice(S // 2, S)]
        xw = keep.tile([P, S], U32, tag="w1_bf16", align_bytes=64)
        for i, half in enumerate(halves):
            nc.vector.tensor_copy(out=xw[:, half], in_=x_word_cols[:].bitcast(U32).indirect(offs_sb[:, 16 * i : 16 * i + 16]))

        w2_stage = keep.tile([P, 2 * W + PACK * N // 2], F32, tag="x_words", align_bytes=64)
        w2_bf16 = w2_stage[:, 2 * W :].bitcast(BF16)
        nc.vector.tensor_copy(out=grouped_view(w2_bf16)[:, : P // 2], in_=dealt_view(w2_low[:]))

        ys = []
        for t in range(PACK):
            acc = psum.tile([P, S], F32, name="y_acc%d" % t)
            cols = slice(t * P, (t + 1) * P)
            for half in halves:
                nc.tensor.matmul_mx(out=acc[:, half], lhsT=w1_codes[:, cols].bitcast(FP8X4), lhsT_scale=w1_scales[:, cols],
                                    rhs=xw[:, half].bitcast(FP8X4), rhs_scale=xs[:, half], start=True, stop=True)
            y = keep.tile([P, S], F32, name="y%d" % t)
            nc.vector.tensor_copy(out=y[:], in_=acc[:])
            ys.append(y)

        nc.vector.tensor_copy(out=grouped_view(w2_bf16)[:, P // 2 :], in_=dealt_view(w2_high[:]))
        w2_codes, w2_scales = quantise(w2_bf16, "w2", "w2_codes")

        last = SLICES - 1
        picked_tiles = [keep.tile([P, 3, PACK, W], F32, name="picked0")[:]]
        middle = keep.tile([P, 2, 3, PACK, W], F32, tag="picked")
        picked_tiles.extend([middle[:, 0], middle[:, 1]])

        def picked(kind, step):
            s, t = divmod(step, PACK)
            return picked_tiles[s][:, kind, t, :]

        nbgs = [w2_stage[:, : PACK * W].rearrange("p (t w) -> p t w", t=PACK)]
        nbgs.extend([keep.tile([P, PACK, W], F32, name="nbg%d" % s)[:] for s in range(1, SLICES)])
        m = keep.tile([P, PACK, W], F32)
        z = keep.tile([P, 2 * W], F32, align_bytes=64)
        z_bf16 = z[:].bitcast(BF16)

        def gather(kind, lst, step, sign):
            s, t = divmod(step, PACK)
            nc.scalar.activation(picked(kind, step), ys[t][:].indirect(lst[:, s * COLS : (s + 1) * COLS]), ACT.Sigmoid, scale=sign)

        def gain(step):
            s, t = divmod(step, PACK)
            if s == 0:
                nc.vector.tensor_scalar(out=nbgs[s][:, t, :], in0=picked(0, step), scalar1=gn_sb[:, t : t + 1], scalar2=None, op0=ALU.mult)
            else:
                nc.scalar.activation(nbgs[s][:, t, :], picked(0, step), ACT.Copy, scale=gn_sb[:, t : t + 1])

        accs = []

        def copy_out(s, t, dst):
            if s == 0:
                nc.vector.tensor_copy(out=dst, in_=accs[s][t])
            else:
                nc.scalar.copy(out=dst, in_=accs[s][t])

        def put(s, t, src):
            nc.vector.tensor_copy(out=pages[t][:].indirect(slot_sb[:, s * COLS : (s + 1) * COLS]), in_=src)
            if s == last:
                nc.sync.dma_start(out=out_rows[:, t, :], in_=pages[t][:])

        gather(0, c2_sb, 0, -1.0)
        gain(0)
        for s in range(SLICES):
            waiting = []

            def hand_on(place, dst):
                while waiting:
                    put(*waiting.pop(0))
                t = place - LAG[s]
                if s > 0 and 0 <= t < (PACK if s < last else PACK - 1):
                    copy_out(s - 1, t, dst)
                    waiting.append((s - 1, t, dst))

            if s == 1:
                spare = keep.tile([P, PACK - 1, W], F32, tag="codes0", align_bytes=64)
            if s == last - 1:
                picked_tiles.append(keep.tile([P, 3, PACK, W], F32, name="picked3", tag="codes1", align_bytes=64)[:])
            for t in range(PACK):
                step = PACK * s + t
                if step + 1 < PACK * SLICES:
                    gather(0, c2_sb, step + 1, -1.0)
                gather(1, c3_sb, step, 1.0)
                gather(2, c1_sb, step, 1.0)
                if step + 1 < PACK * SLICES:
                    gain(step + 1)
                c, a = picked(1, step), picked(2, step)
                sg = spare[:, t - 1, :] if s == 1 and t > 0 else m[:, t, :]
                nc.vector.scalar_tensor_tensor(out=sg, in0=c, scalar=gn_sb[:, t : t + 1], in1=nbgs[s][:, t, :], op0=ALU.mult, op1=ALU.add)
                if t == 0 and s > 0:
                    hand_on(0, picked(0, step - PACK))
                    hand_on(1, picked(0, step - PACK + 1))
                else:
                    hand_on(-1, None)
                nc.vector.tensor_tensor(out=m[:, t, :], in0=a, in1=sg, op=ALU.mult)
                hand_on(t + 1 if t > 0 else -1, a)
            nc.vector.tensor_tensor(out=z_bf16.rearrange("p (g i t) -> p g t i", i=4, t=PACK), in0=nbgs[s].rearrange("p t (g i) -> p g t i", i=4),
                                    in1=m[:].rearrange("p t (g i) -> p g t i", i=4), op=ALU.subtract)
            hand_on(PACK + 1, nbgs[s][:, 0, :])
            z_codes = keep.tile([P, W], U32, name="z_codes", tag="codes%d" % s, align_bytes=64)
            z_scales = ring.tile([P, W], U8, name="z_scales", align_bytes=64)
            nc.vector.quantize_mx(out=z_codes[:].bitcast(FP8X4), scales=z_scales[:], in_=z_bf16)
            if s < last:
                bank = psum_h.tile([P, PACK, W], F32, name="h_acc")
                acc = [bank[:, t, :] for t in range(PACK)]
            else:
                acc = [psum.tile([P, W], F32, name="y_acc%d" % t)[:] for t in range(PACK)]
            accs.append(acc)
            for t in range(PACK):
                wc = slice(t * P, (t + 1) * P)
                nc.tensor.matmul_mx(out=acc[t], lhsT=w2_codes[:, wc].bitcast(FP8X4), lhsT_scale=w2_scales[:, wc],
                                    rhs=z_codes[:].bitcast(FP8X4), rhs_scale=z_scales[:], start=True, stop=True)
            hand_on(-1, None)
        for t in range(PACK):
            if t == PACK - 1:
                late = picked(1, PACK * last)
                copy_out(last - 1, t, late)
                put(last - 1, t, late)
            dst = picked(1, PACK * last + t)
            copy_out(last, t, dst)
            put(last, t, dst)
